import numpy as np
import ml_dtypes


def mxq(x, axis, fmt="e4m3"):
    dtype, down = {"e4m3": (ml_dtypes.float8_e4m3fn, 7), "e5m2": (ml_dtypes.float8_e5m2, 14)}[fmt]
    v = np.moveaxis(np.asarray(x, np.float32).astype(ml_dtypes.bfloat16).astype(np.float64), axis, -1)
    blocks = v.reshape(v.shape[:-1] + (-1, 32))
    amax = np.abs(blocks).max(-1, keepdims=True)
    byte = np.maximum(np.where(amax > 0, np.frexp(amax)[1] - 1 + 127, 0) - down, 1)
    scale = np.exp2(byte - 127.0)
    codes = (blocks / scale).astype(np.float32).astype(dtype).astype(np.float64)
    return np.moveaxis((codes * scale).reshape(v.shape), -1, axis)


WIDE = False


def mx_kscale(k):
    if not WIDE:
        return np.ones(k)
    levels = np.array([10, -10, 5, -5, 0])
    if k % 512:
        return np.exp2(np.random.permutation(np.resize(levels, k // 32))).repeat(32)
    a = np.empty((k // 512, 16))
    for p in range(k // 512):
        a[p, :8] = np.random.permutation(np.resize(levels, 8))
        for g in range(8):
            far = levels[np.abs(levels - a[p, g]) >= 10]
            a[p, g + 8] = far[np.random.randint(len(far))]
    return np.exp2(a.ravel()).repeat(32)


def f64(x):
    return np.asarray(x).astype(np.float64)


def striped(idx):
    return np.tile(idx.reshape(-1, 16).T, (8, 1)).astype(np.uint16)


def unstriped(offs):
    return offs[:16].T.reshape(-1).astype(np.int64)


def striped8(idx):
    return np.concatenate([x.reshape(-1, 16).T for x in idx]).astype(np.uint16)


def runs(offs, k):
    lists = np.stack([offs[16 * r : 16 * r + 16].T.reshape(-1) for r in range(8)]).astype(np.int64)
    return lists[np.arange(k) % 512 // 64]


def pack_weight(w):
    k, n = w.shape
    w = f64(np.asarray(w, np.float32).astype(ml_dtypes.bfloat16)).reshape(k // 32, 32, n)
    amax = np.abs(w).max(1)
    byte = np.clip(np.where(amax > 0, np.frexp(amax)[1] - 1 + 127 - 7, 1), 1, 254)
    scaled = (w * np.exp2(127.0 - byte)[:, None, :]).reshape(k, n).astype(np.float32)
    words = np.ascontiguousarray(scaled.reshape(k // 512, 128, 4, n).transpose(0, 1, 3, 2)).astype(ml_dtypes.float8_e4m3fn).view(np.uint8)
    return words, np.ascontiguousarray(byte.astype(np.uint8).reshape(k // 512, 16, n))


def unpack_weight(words, scales):
    g, p, n, _ = words.shape
    vals = np.ascontiguousarray(words).view(ml_dtypes.float8_e4m3fn).astype(np.float64) * np.repeat(np.exp2(scales.astype(np.float64) - 127.0), 8, axis=1)[..., None]
    return vals.transpose(0, 1, 3, 2).reshape(g * 512, n)

def planes(y):
    n, m = y.shape
    v = y.astype(np.float32).astype(ml_dtypes.bfloat16).astype(np.float64).reshape(n // 32, 32, m)
    top = np.abs(v).max(1)
    byte = np.clip(np.where(top > 0, np.frexp(top)[1] - 1 + 127 - 7, 1), 1, 254)
    codes = (v * np.exp2(127.0 - byte)[:, None, :]).reshape(n, m).astype(np.float32).astype(ml_dtypes.float8_e4m3fn).view(np.uint8)
    words = codes.reshape(n // 512, 128, 4, m).transpose(0, 1, 3, 2)
    return np.ascontiguousarray(words), np.ascontiguousarray(byte.astype(np.uint8).reshape(n // 512, 16, m))


K, T, S, N, H, W, C = 512, 2048, 256, 512, 512, 128, 512


def setup_inputs():
    n = np.random.standard_normal
    s = mx_kscale(K)[:, None]
    u = mx_kscale(K)
    packed_xT = pack_weight(n((K, T)) * s)
    packed_w1 = pack_weight(n((K, H)) / np.sqrt(K) / s)
    packed_w2 = pack_weight(n((K, H)) / np.sqrt(K) / s)
    packed_w3 = pack_weight(n((H, N)) / np.sqrt(H) / u[:, None])
    perm = np.random.permutation(S)
    return {
        "x_words": packed_xT[0],
        "x_scales": packed_xT[1],
        "w1_words": packed_w1[0],
        "w1_scales": packed_w1[1],
        "w2_words": packed_w2[0],
        "w2_scales": packed_w2[1],
        "gn": (np.random.uniform(0.5, 1.5, (H, 1)) * u[:, None]).astype(np.float32),
        "w3_words": packed_w3[0],
        "w3_scales": packed_w3[1],
        "gs": (np.random.uniform(0.5, 1.5, (K, 1)) / s).astype(np.float32),
        "offs": striped(np.random.permutation(T)[:S]),
        "two": striped(np.random.permutation(T)[:S]),
        "n1": striped8(np.stack([np.random.permutation(S) for _ in range(8)])),
        "n2": striped8(np.stack([np.random.permutation(S) for _ in range(8)])),
        "n3": striped8(np.stack([np.random.permutation(S) for _ in range(8)])),
        "n4": striped(perm[:W]),
        "n5": striped(perm[W:]),
        "cand": striped(np.random.permutation(T)[:C]),
        "n6": striped(np.random.permutation(S)[:W]),
        "n7": striped(np.random.permutation(S)[:W]),
    }


def reference(x_words, x_scales, w1_words, w1_scales, w2_words, w2_scales, gn, w3_words, w3_scales, gs, offs, two, n1, n2, n3, n4, n5, cand, n6, n7):
    x_cand = unpack_weight(x_words, x_scales)[:, unstriped(cand)]
    x_two = unpack_weight(x_words, x_scales)[:, unstriped(two)]
    d = unpack_weight(w2_words, w2_scales).T @ x_two
    pa = d[:, unstriped(n4)]
    pb = d[:, unstriped(n5)]
    rb = pa * pb
    ra = pa + pb
    ds = np.zeros((H, S))
    ds[:, unstriped(n4)] = ra
    dt = ds.copy()
    dt[:, unstriped(n5)] = rb
    z2 = f64(gs) * dt
    b = 0.0625 * ((x_cand.T @ mxq(z2, 0, "e4m3")))
    xq = unpack_weight(x_words, x_scales)[:, unstriped(offs)]
    y = unpack_weight(w1_words, w1_scales).T @ xq
    z = f64(gn) * (np.maximum(y, y[np.arange(H)[:, None], runs(n1, H)]) - (np.maximum(y[np.arange(H)[:, None], runs(n2, H)], y[np.arange(H)[:, None], runs(n3, H)])))
    a = unpack_weight(w3_words, w3_scales).T @ mxq(z, 0, "e4m3")
    ra2 = b[:, unstriped(n7)] - (0.5 * a[:, unstriped(n6)])
    out = a.copy()
    out[:, unstriped(n6)] = ra2
    return (out,) + planes(out)

@@ -1,0 +1,232 @@
+from contextlib import ExitStack
+
+import concourse.mybir as mybir
+
+K, T, S, W, C = 512, 2048, 256, 128, 512
+FLOPS = 2 * K * 512 * S * 4
+
+F32 = mybir.dt.float32
+BF16 = mybir.dt.bfloat16
+I32 = mybir.dt.int32
+U32 = mybir.dt.uint32
+U16 = mybir.dt.uint16
+U8 = mybir.dt.uint8
+FP8X4 = mybir.dt.float8_e4m3fn_x4
+ALU = mybir.AluOpType
+COPY = mybir.ActivationFunctionType.Copy
+
+P = 128
+PACK = 4
+QUADS = 4
+LINE = 16
+
+
+def word_view(dram_words):
+    return dram_words[0].rearrange("p n t -> p (n t)").bitcast(I32)
+
+
+def load_scales(queue, plane, first_row, dram_scales, quads=range(QUADS)):
+    for q in quads:
+        rows = slice(32 * q + first_row, 32 * q + first_row + 4)
+        queue.dma_start(plane[rows, :].bitcast(I32), dram_scales[0, 4 * q : 4 * q + 4, :].bitcast(I32))
+
+
+def deal(nc, dst, src, run):
+    nc.vector.tensor_copy(
+        dst.rearrange("p (t c i) -> p c t i", t=PACK, i=run),
+        src.rearrange("p (c i t) -> p c t i", t=PACK, i=run),
+    )
+
+
+def tile_picked_tfcdputbmixbond_none_po_kernel(
+    tc, x_words, x_scales, w1_words, w1_scales, w2_words, w2_scales, gn, w3_words, w3_scales, gs,
+    offs, two, n1, n2, n3, n4, n5, cand, n6, n7, out_0, out_1, out_2,
+):
+    nc = tc.nc
+    with ExitStack() as ctx:
+        lists = ctx.enter_context(tc.tile_pool(name="lists", bufs=1))
+        keep = ctx.enter_context(tc.tile_pool(name="keep", bufs=1))
+        psum = ctx.enter_context(tc.psum_pool(name="psum", bufs=1))
+
+        def sb(name, shape, dtype):
+            return keep.tile(shape, dtype, name=name, align_bytes=64)
+
+        def load_list(name, dram):
+            held = lists.tile(list(dram.shape), U16, name=name)
+            nc.sync.dma_start(held[:], dram)
+            return held
+
+        def load_words(queue, name, dram, width):
+            held = sb(name, [P, width], I32)
+            queue.dma_start(held[:], word_view(dram))
+            return held
+
+        def product(bank, stat_words, stat_scales, first_row, t, mov_words, mov_scales):
+            acc = psum.tile([P, S], F32, name="acc", tag="bank%d" % bank)
+            cols = slice(P * t, P * (t + 1))
+            nc.tensor.matmul_mx(
+                acc[:], lhsT=stat_words[:, cols].bitcast(FP8X4), lhsT_scale=stat_scales[first_row:P, cols],
+                rhs=mov_words[:].bitcast(FP8X4), rhs_scale=mov_scales[:], start=True, stop=True,
+            )
+            return acc
+
+        def pick_scales(name, offsets, count):
+            scales = sb(name + "_scales", [P, count], U8)
+            nc.vector.tensor_copy(scales[:], xs[:].indirect(offsets[:]))
+            return scales
+
+        def pick_words(name, offsets, count):
+            words = sb(name + "_words", [P, count], I32)
+            nc.vector.tensor_copy(words[:].bitcast(U32), xw[:].bitcast(U32).indirect(offsets[:]))
+            return words
+
+        def pick(name, offsets, count):
+            scales = pick_scales(name, offsets, count)
+            return pick_words(name, offsets, count), scales
+
+        def fetch(dst, window, offsets):
+            nc.scalar.activation(dst, window[:].indirect(offsets[:]), COPY)
+
+        def put(window, offsets, src):
+            nc.scalar.activation(window[:].indirect(offsets[:]), src, COPY)
+
+        def quantise(name, grouped):
+            words = sb(name + "_words", [P, S], I32)
+            scales = sb(name + "_scales", [P, S], U8)
+            nc.vector.quantize_mx(words[:].bitcast(FP8X4), scales[:], grouped[:].rearrange("p s t -> p (s t)"))
+            return words, scales
+
+        xs = sb("xs", [P, T], U8)
+        w1s_raw = sb("w1s_raw", [P, K], U8)
+        w23s_raw = sb("w23s_raw", [P, K], U8)
+        nc.vector.memset(xs[:].bitcast(I32), 0)
+        nc.gpsimd.memset(w1s_raw[:].bitcast(I32), 0)
+        nc.vector.memset(w23s_raw[:].bitcast(I32), 0)
+        y = [sb("y%d" % t, [P, 2 * S], F32) for t in range(PACK)]
+        for t in range(PACK):
+            nc.vector.memset(y[t][:, S:], 0.0)
+
+        w1w_raw = load_words(nc.sync, "w1w_raw", w1_words, K)
+        offs_l = load_list("offs_l", offs)
+        n1_l = load_list("n1_l", n1)
+        xw = load_words(nc.sync, "xw", x_words, T)
+        load_scales(nc.scalar, xs, 0, x_scales)
+        load_scales(nc.sync, w1s_raw, 0, w1_scales, range(0, 2))
+        load_scales(nc.gpsimd, w1s_raw, 0, w1_scales, range(2, 4))
+        n2_l = load_list("n2_l", n2)
+        n3_l = load_list("n3_l", n3)
+        two_l = load_list("two_l", two)
+        w2w_raw = load_words(nc.sync, "w2w_raw", w2_words, K)
+        load_scales(nc.sync, w23s_raw, 0, w2_scales)
+        load_scales(nc.sync, w23s_raw, 4, w3_scales)
+        n4_l = load_list("n4_l", n4)
+        n5_l = load_list("n5_l", n5)
+        gn_t = sb("gn_t", [P, PACK], F32)
+        gs_t = sb("gs_t", [P, PACK], F32)
+        nc.sync.dma_start(gn_t[:], gn.rearrange("(p t) o -> p (t o)", t=PACK))
+        cand_l = load_list("cand_l", cand)
+        w3w_raw = load_words(nc.sync, "w3w_raw", w3_words, K)
+        nc.sync.dma_start(gs_t[:], gs.rearrange("(p t) o -> p (t o)", t=PACK))
+        n6_l = load_list("n6_l", n6)
+        n7_l = load_list("n7_l", n7)
+
+        w1w = sb("w1w", [P, K], I32)
+        w1s = sb("w1s", [P, K], U8)
+        deal(nc, w1w[:], w1w_raw[:], LINE // 4)
+        xq_scales = pick_scales("xq", offs_l, S)
+        deal(nc, w1s[:], w1s_raw[:], LINE)
+        xq_words = pick_words("xq", offs_l, S)
+        for t in range(PACK):
+            acc = product(t, w1w, w1s, 0, t, xq_words, xq_scales)
+            if t == 0:
+                nc.scalar.copy(y[t][:, :S], acc[:])
+            else:
+                nc.vector.tensor_copy(y[t][:, :S], acc[:])
+        g1 = sb("g1", [P, PACK, S], F32)
+        g2 = sb("g2", [P, PACK, S], F32)
+        g3 = sb("g3", [P, PACK, S], F32)
+        for t in range(PACK):
+            fetch(g1[:, t, :], y[t], n1_l)
+            fetch(g2[:, t, :], y[t], n2_l)
+            fetch(g3[:, t, :], y[t], n3_l)
+
+        xt_words, xt_scales = pick("xt", two_l, S)
+        w2w = sb("w2w", [P, K], I32)
+        w23s = sb("w23s", [P, K], U8)
+        deal(nc, w2w[:], w2w_raw[:], LINE // 4)
+        deal(nc, w23s[:], w23s_raw[:], LINE)
+        d = [sb("d%d" % t, [P, S], F32) for t in range(PACK)]
+        for t in range(PACK):
+            acc = product(PACK + t, w2w, w23s, 0, t, xt_words, xt_scales)
+            nc.vector.tensor_copy(d[t][:], acc[:])
+        pa = sb("pa", [P, PACK, W], F32)
+        pb = sb("pb", [P, PACK, W], F32)
+        ra = sb("ra", [P, PACK, W], F32)
+        rb = sb("rb", [P, PACK, W], F32)
+        for t in range(PACK):
+            fetch(pa[:, t, :], d[t], n4_l)
+            fetch(pb[:, t, :], d[t], n5_l)
+        dt_tiles = [sb("dt%d" % t, [P, S], F32) for t in range(PACK)]
+        for pair in (slice(0, 2), slice(2, 4)):
+            nc.vector.tensor_tensor(ra[:, pair, :], pa[:, pair, :], pb[:, pair, :], ALU.add)
+            nc.vector.tensor_tensor(rb[:, pair, :], pa[:, pair, :], pb[:, pair, :], ALU.mult)
+        for pair in (slice(0, 2), slice(2, 4)):
+            for t in range(pair.start, pair.stop):
+                put(dt_tiles[t], n4_l, ra[:, t, :])
+            for t in range(pair.start, pair.stop):
+                put(dt_tiles[t], n5_l, rb[:, t, :])
+
+        hi = sb("hi", [P, PACK, S], F32)
+        lo = sb("lo", [P, PACK, S], F32)
+        z_grouped = sb("z_grouped", [P, S, PACK], BF16)
+        for t in range(PACK):
+            nc.vector.tensor_tensor(hi[:, t, :], y[t][:, :S], g1[:, t, :], ALU.max)
+            nc.vector.tensor_tensor(lo[:, t, :], g2[:, t, :], g3[:, t, :], ALU.max)
+            nc.vector.tensor_tensor(hi[:, t, :], hi[:, t, :], lo[:, t, :], ALU.subtract)
+            nc.vector.tensor_scalar(z_grouped[:, :, t], hi[:, t, :], gn_t[:, t : t + 1], None, ALU.mult)
+        z_words, z_scales = quantise("z", z_grouped)
+        w3w = sb("w3w", [P, K], I32)
+        deal(nc, w3w[:], w3w_raw[:], LINE // 4)
+        a = [sb("a%d" % t, [P, S], F32) for t in range(PACK)]
+        for t in range(PACK):
+            acc = product(t, w3w, w23s, 4, t, z_words, z_scales)
+            nc.vector.tensor_copy(a[t][:], acc[:])
+
+        xc_words_raw, xc_scales_raw = pick("xc", cand_l, C)
+        xc_words = sb("xc_words_dealt", [P, C], I32)
+        xc_scales = sb("xc_scales_dealt", [P, C], U8)
+        deal(nc, xc_words[:], xc_words_raw[:], LINE // 4)
+        deal(nc, xc_scales[:], xc_scales_raw[:], LINE)
+
+        ga = sb("ga", [P, PACK, W], F32)
+        for t in range(PACK):
+            fetch(ga[:, t, :], a[t], n6_l)
+
+        z2_grouped = sb("z2_grouped", [P, S, PACK], BF16)
+        for t in range(PACK):
+            nc.vector.tensor_scalar(z2_grouped[:, :, t], dt_tiles[t][:], gs_t[:, t : t + 1], None, ALU.mult)
+        z2_words, z2_scales = quantise("z2", z2_grouped)
+        b = [sb("b%d" % t, [P, S], F32) for t in range(PACK)]
+        for t in range(PACK):
+            acc = product(PACK + t, xc_words, xc_scales, 0, t, z2_words, z2_scales)
+            if t == 0:
+                nc.scalar.activation(b[t][:], acc[:], COPY, scale=0.0625)
+            else:
+                nc.vector.tensor_scalar(b[t][:], acc[:], 0.0625, None, ALU.mult)
+
+        gb = sb("gb", [P, PACK, W], F32)
+        ra2 = sb("ra2", [P, PACK, W], F32)
+        out_grouped = sb("out_grouped", [P, S, PACK], BF16)
+        out_rows = out_0.rearrange("(p t) s -> p t s", t=PACK)
+        for t in range(PACK):
+            fetch(gb[:, t, :], b[t], n7_l)
+            nc.vector.scalar_tensor_tensor(ra2[:, t, :], ga[:, t, :], -0.5, gb[:, t, :], ALU.mult, ALU.add)
+            put(a[t], n6_l, ra2[:, t, :])
+        for t in range(PACK):
+            nc.sync.dma_start(out_rows[:, t, :], a[t][:])
+            nc.vector.tensor_copy(out_grouped[:, :, t], a[t][:])
+        out_words, out_scales = quantise("out", out_grouped)
+        nc.sync.dma_start(word_view(out_1), out_words[:])
+        for q in range(QUADS):
+            queue = nc.scalar if q % 2 == 0 else nc.sync
+            queue.dma_start(out_2[0, 4 * q : 4 * q + 4, :].bitcast(I32), out_scales[32 * q : 32 * q + 4, :].bitcast(I32))

@@ -31,8 +31,8 @@ def load_scales(queue, plane, first_row, dram_scales, quads=range(QUADS)):
         queue.dma_start(plane[rows, :].bitcast(I32), dram_scales[0, 4 * q : 4 * q + 4, :].bitcast(I32))
 
 
-def deal(nc, dst, src, run):
-    nc.vector.tensor_copy(
+def deal(engine, dst, src, run):
+    engine.tensor_copy(
         dst.rearrange("p (t c i) -> p c t i", t=PACK, i=run),
         src.rearrange("p (c i t) -> p c t i", t=PACK, i=run),
     )
@@ -48,8 +48,8 @@ def tile_picked_tfcdputbmixbond_none_po_kernel(
         keep = ctx.enter_context(tc.tile_pool(name="keep", bufs=1))
         psum = ctx.enter_context(tc.psum_pool(name="psum", bufs=1))
 
-        def sb(name, shape, dtype):
-            return keep.tile(shape, dtype, name=name, align_bytes=64)
+        def sb(name, shape, dtype, tag=None):
+            return keep.tile(shape, dtype, name=name, tag=tag or name, align_bytes=64)
 
         def load_list(name, dram):
             held = lists.tile(list(dram.shape), U16, name=name)
@@ -61,13 +61,14 @@ def tile_picked_tfcdputbmixbond_none_po_kernel(
             queue.dma_start(held[:], word_view(dram))
             return held
 
-        def product(bank, stat_words, stat_scales, first_row, t, mov_words, mov_scales):
+        def product(bank, stat_words, stat_scales, t, mov_words, mov_scales, spans):
             acc = psum.tile([P, S], F32, name="acc", tag="bank%d" % bank)
-            cols = slice(P * t, P * (t + 1))
-            nc.tensor.matmul_mx(
-                acc[:], lhsT=stat_words[:, cols].bitcast(FP8X4), lhsT_scale=stat_scales[first_row:P, cols],
-                rhs=mov_words[:].bitcast(FP8X4), rhs_scale=mov_scales[:], start=True, stop=True,
-            )
+            rows = slice(P * t, P * (t + 1))
+            for cols in spans:
+                nc.tensor.matmul_mx(
+                    acc[:, cols], lhsT=stat_words[:, rows].bitcast(FP8X4), lhsT_scale=stat_scales[:, rows],
+                    rhs=mov_words[:, cols].bitcast(FP8X4), rhs_scale=mov_scales[:, cols], start=True, stop=True,
+                )
             return acc
 
         def pick_scales(name, offsets, count):
@@ -90,18 +91,23 @@ def tile_picked_tfcdputbmixbond_none_po_kernel(
         def put(window, offsets, src):
             nc.scalar.activation(window[:].indirect(offsets[:]), src, COPY)
 
-        def quantise(name, grouped):
+        def quantise(name, grouped, spans):
             words = sb(name + "_words", [P, S], I32)
             scales = sb(name + "_scales", [P, S], U8)
-            nc.vector.quantize_mx(words[:].bitcast(FP8X4), scales[:], grouped[:].rearrange("p s t -> p (s t)"))
+            for cols in spans:
+                nc.vector.quantize_mx(
+                    words[:, cols].bitcast(FP8X4), scales[:, cols], grouped[:, cols, :].rearrange("p s t -> p (s t)")
+                )
             return words, scales
 
         xs = sb("xs", [P, T], U8)
         w1s_raw = sb("w1s_raw", [P, K], U8)
-        w23s_raw = sb("w23s_raw", [P, K], U8)
+        w2s_raw = sb("w2s_raw", [P, K], U8)
+        w3s_raw = sb("w3s_raw", [P, K], U8)
         nc.vector.memset(xs[:].bitcast(I32), 0)
         nc.gpsimd.memset(w1s_raw[:].bitcast(I32), 0)
-        nc.vector.memset(w23s_raw[:].bitcast(I32), 0)
+        nc.vector.memset(w2s_raw[:].bitcast(I32), 0)
+        nc.vector.memset(w3s_raw[:].bitcast(I32), 0)
         y = [sb("y%d" % t, [P, 2 * S], F32) for t in range(PACK)]
         for t in range(PACK):
             nc.vector.memset(y[t][:, S:], 0.0)
@@ -117,27 +123,27 @@ def tile_picked_tfcdputbmixbond_none_po_kernel(
         n3_l = load_list("n3_l", n3)
         two_l = load_list("two_l", two)
         w2w_raw = load_words(nc.sync, "w2w_raw", w2_words, K)
-        load_scales(nc.sync, w23s_raw, 0, w2_scales)
-        load_scales(nc.sync, w23s_raw, 4, w3_scales)
-        n4_l = load_list("n4_l", n4)
-        n5_l = load_list("n5_l", n5)
+        load_scales(nc.sync, w2s_raw, 0, w2_scales)
+        cand_l = load_list("cand_l", cand)
         gn_t = sb("gn_t", [P, PACK], F32)
         gs_t = sb("gs_t", [P, PACK], F32)
         nc.sync.dma_start(gn_t[:], gn.rearrange("(p t) o -> p (t o)", t=PACK))
-        cand_l = load_list("cand_l", cand)
+        n4_l = load_list("n4_l", n4)
+        n5_l = load_list("n5_l", n5)
         w3w_raw = load_words(nc.sync, "w3w_raw", w3_words, K)
+        load_scales(nc.sync, w3s_raw, 0, w3_scales)
         nc.sync.dma_start(gs_t[:], gs.rearrange("(p t) o -> p (t o)", t=PACK))
         n6_l = load_list("n6_l", n6)
         n7_l = load_list("n7_l", n7)
 
         w1w = sb("w1w", [P, K], I32)
         w1s = sb("w1s", [P, K], U8)
-        deal(nc, w1w[:], w1w_raw[:], LINE // 4)
+        deal(nc.vector, w1w[:], w1w_raw[:], LINE // 4)
         xq_scales = pick_scales("xq", offs_l, S)
-        deal(nc, w1s[:], w1s_raw[:], LINE)
+        deal(nc.vector, w1s[:], w1s_raw[:], LINE)
         xq_words = pick_words("xq", offs_l, S)
         for t in range(PACK):
-            acc = product(t, w1w, w1s, 0, t, xq_words, xq_scales)
+            acc = product(t, w1w, w1s, t, xq_words, xq_scales, [slice(0, S)])
             if t == 0:
                 nc.scalar.copy(y[t][:, :S], acc[:])
             else:
@@ -152,12 +158,16 @@ def tile_picked_tfcdputbmixbond_none_po_kernel(
 
         xt_words, xt_scales = pick("xt", two_l, S)
         w2w = sb("w2w", [P, K], I32)
-        w23s = sb("w23s", [P, K], U8)
-        deal(nc, w2w[:], w2w_raw[:], LINE // 4)
-        deal(nc, w23s[:], w23s_raw[:], LINE)
+        w2s = sb("w2s", [P, K], U8)
+        deal(nc.vector, w2w[:], w2w_raw[:], LINE // 4)
+        deal(nc.vector, w2s[:], w2s_raw[:], LINE)
+        w3w = sb("w3w", [P, K], I32)
+        w3s = sb("w3s", [P, K], U8)
+        deal(nc.vector, w3w[:], w3w_raw[:], LINE // 4)
+        deal(nc.vector, w3s[:], w3s_raw[:], LINE)
         d = [sb("d%d" % t, [P, S], F32) for t in range(PACK)]
         for t in range(PACK):
-            acc = product(PACK + t, w2w, w23s, 0, t, xt_words, xt_scales)
+            acc = product(PACK + t, w2w, w2s, t, xt_words, xt_scales, [slice(0, S)])
             nc.vector.tensor_copy(d[t][:], acc[:])
         pa = sb("pa", [P, PACK, W], F32)
         pb = sb("pb", [P, PACK, W], F32)
@@ -167,48 +177,59 @@ def tile_picked_tfcdputbmixbond_none_po_kernel(
             fetch(pa[:, t, :], d[t], n4_l)
             fetch(pb[:, t, :], d[t], n5_l)
         dt_tiles = [sb("dt%d" % t, [P, S], F32) for t in range(PACK)]
-        for pair in (slice(0, 2), slice(2, 4)):
+
+        def pair_up(pair):
             nc.vector.tensor_tensor(ra[:, pair, :], pa[:, pair, :], pb[:, pair, :], ALU.add)
             nc.vector.tensor_tensor(rb[:, pair, :], pa[:, pair, :], pb[:, pair, :], ALU.mult)
-        for pair in (slice(0, 2), slice(2, 4)):
             for t in range(pair.start, pair.stop):
                 put(dt_tiles[t], n4_l, ra[:, t, :])
             for t in range(pair.start, pair.stop):
                 put(dt_tiles[t], n5_l, rb[:, t, :])
 
-        hi = sb("hi", [P, PACK, S], F32)
-        lo = sb("lo", [P, PACK, S], F32)
-        z_grouped = sb("z_grouped", [P, S, PACK], BF16)
-        for t in range(PACK):
-            nc.vector.tensor_tensor(hi[:, t, :], y[t][:, :S], g1[:, t, :], ALU.max)
-            nc.vector.tensor_tensor(lo[:, t, :], g2[:, t, :], g3[:, t, :], ALU.max)
-            nc.vector.tensor_tensor(hi[:, t, :], hi[:, t, :], lo[:, t, :], ALU.subtract)
-            nc.vector.tensor_scalar(z_grouped[:, :, t], hi[:, t, :], gn_t[:, t : t + 1], None, ALU.mult)
-        z_words, z_scales = quantise("z", z_grouped)
-        w3w = sb("w3w", [P, K], I32)
-        deal(nc, w3w[:], w3w_raw[:], LINE // 4)
-        a = [sb("a%d" % t, [P, S], F32) for t in range(PACK)]
-        for t in range(PACK):
-            acc = product(t, w3w, w23s, 4, t, z_words, z_scales)
-            nc.vector.tensor_copy(a[t][:], acc[:])
+        z_planes = sb("z_planes", [P, PACK, S], BF16)
+
+        def z_rows(planes, work):
+            for j, t in enumerate(planes):
+                nc.vector.tensor_tensor(work[:, 0, j, :], g2[:, t, :], g3[:, t, :], ALU.max)
+                nc.vector.tensor_tensor(work[:, 1, j, :], y[t][:, :S], g1[:, t, :], ALU.max)
+            for j, t in enumerate(planes):
+                nc.vector.tensor_tensor(work[:, 0, j, :], work[:, 1, j, :], work[:, 0, j, :], ALU.subtract)
+            for j, t in enumerate(planes):
+                nc.vector.tensor_scalar(z_planes[:, t, :], work[:, 0, j, :], gn_t[:, t : t + 1], None, ALU.mult)
 
         xc_words_raw, xc_scales_raw = pick("xc", cand_l, C)
-        xc_words = sb("xc_words_dealt", [P, C], I32)
-        xc_scales = sb("xc_scales_dealt", [P, C], U8)
-        deal(nc, xc_words[:], xc_words_raw[:], LINE // 4)
-        deal(nc, xc_scales[:], xc_scales_raw[:], LINE)
+        z_rows((0, 1), sb("work_early", [P, 2, 2, S], F32))
+        pair_up(slice(0, 2))
+        z_rows((2, 3), sb("work_late", [P, 2, 2, S], F32, tag="w2w"))
+        pair_up(slice(2, 4))
+        z_grouped = sb("z_grouped", [P, S, PACK], BF16)
+        nc.vector.tensor_copy(
+            z_grouped[:].rearrange("p (c i) t -> p c t i", i=2), z_planes[:].rearrange("p t (c i) -> p c t i", i=2)
+        )
+        z_words, z_scales = quantise("z", z_grouped, [slice(0, S)])
+        a = [sb("a%d" % t, [P, S], F32) for t in range(PACK)]
+        for t in range(PACK):
+            acc = product(t, w3w, w3s, t, z_words, z_scales, [slice(0, S)])
+            nc.vector.tensor_copy(a[t][:], acc[:])
+
+        xc_words = sb("xc_words_dealt", [P, C], I32, tag="z_grouped")
+        xc_scales = sb("xc_scales_dealt", [P, C], U8, tag="z_planes")
+        deal(nc.vector, xc_words[:], xc_words_raw[:], LINE // 4)
+        deal(nc.vector, xc_scales[:], xc_scales_raw[:], LINE)
 
         ga = sb("ga", [P, PACK, W], F32)
         for t in range(PACK):
             fetch(ga[:, t, :], a[t], n6_l)
 
+        halves = [slice(0, S // 2), slice(S // 2, S)]
         z2_grouped = sb("z2_grouped", [P, S, PACK], BF16)
         for t in range(PACK):
-            nc.vector.tensor_scalar(z2_grouped[:, :, t], dt_tiles[t][:], gs_t[:, t : t + 1], None, ALU.mult)
-        z2_words, z2_scales = quantise("z2", z2_grouped)
+            for cols in halves if t == PACK - 1 else [slice(0, S)]:
+                nc.vector.tensor_scalar(z2_grouped[:, cols, t], dt_tiles[t][:, cols], gs_t[:, t : t + 1], None, ALU.mult)
+        z2_words, z2_scales = quantise("z2", z2_grouped, halves)
         b = [sb("b%d" % t, [P, S], F32) for t in range(PACK)]
         for t in range(PACK):
-            acc = product(PACK + t, xc_words, xc_scales, 0, t, z2_words, z2_scales)
+            acc = product(PACK + t, xc_words, xc_scales, t, z2_words, z2_scales, halves)
             if t == 0:
                 nc.scalar.activation(b[t][:], acc[:], COPY, scale=0.0625)
             else:
@@ -224,8 +245,9 @@ def tile_picked_tfcdputbmixbond_none_po_kernel(
             put(a[t], n6_l, ra2[:, t, :])
         for t in range(PACK):
             nc.sync.dma_start(out_rows[:, t, :], a[t][:])
-            nc.vector.tensor_copy(out_grouped[:, :, t], a[t][:])
-        out_words, out_scales = quantise("out", out_grouped)
+            for cols in halves if t == PACK - 1 else [slice(0, S)]:
+                nc.vector.tensor_copy(out_grouped[:, cols, t], a[t][:, cols])
+        out_words, out_scales = quantise("out", out_grouped, halves)
         nc.sync.dma_start(word_view(out_1), out_words[:])
         for q in range(QUADS):
             queue = nc.scalar if q % 2 == 0 else nc.sync

@@ -31,10 +31,10 @@ def load_scales(queue, plane, first_row, dram_scales, quads=range(QUADS)):
         queue.dma_start(plane[rows, :].bitcast(I32), dram_scales[0, 4 * q : 4 * q + 4, :].bitcast(I32))
 
 
-def deal(engine, dst, src, run):
+def deal(engine, dst, src, run, slots=slice(0, PACK)):
     engine.tensor_copy(
-        dst.rearrange("p (t c i) -> p c t i", t=PACK, i=run),
-        src.rearrange("p (c i t) -> p c t i", t=PACK, i=run),
+        dst.rearrange("p (t c i) -> p c t i", t=PACK, i=run)[:, :, slots, :],
+        src.rearrange("p (c i t) -> p c t i", t=PACK, i=run)[:, :, slots, :],
     )
 
 
@@ -104,8 +104,8 @@ def tile_picked_tfcdputbmixbond_none_po_kernel(
         w1s_raw = sb("w1s_raw", [P, K], U8)
         w2s_raw = sb("w2s_raw", [P, K], U8)
         w3s_raw = sb("w3s_raw", [P, K], U8)
-        nc.vector.memset(xs[:].bitcast(I32), 0)
         nc.gpsimd.memset(w1s_raw[:].bitcast(I32), 0)
+        nc.vector.memset(xs[:].bitcast(I32), 0)
         nc.vector.memset(w2s_raw[:].bitcast(I32), 0)
         nc.vector.memset(w3s_raw[:].bitcast(I32), 0)
         y = [sb("y%d" % t, [P, 2 * S], F32) for t in range(PACK)]
@@ -115,11 +115,11 @@ def tile_picked_tfcdputbmixbond_none_po_kernel(
         w1w_raw = load_words(nc.sync, "w1w_raw", w1_words, K)
         offs_l = load_list("offs_l", offs)
         n1_l = load_list("n1_l", n1)
-        xw = load_words(nc.sync, "xw", x_words, T)
-        load_scales(nc.scalar, xs, 0, x_scales)
-        load_scales(nc.sync, w1s_raw, 0, w1_scales, range(0, 2))
-        load_scales(nc.gpsimd, w1s_raw, 0, w1_scales, range(2, 4))
         n2_l = load_list("n2_l", n2)
+        load_scales(nc.sync, w1s_raw, 0, w1_scales, range(0, 2))
+        xw = load_words(nc.sync, "xw", x_words, T)
+        load_scales(nc.sync, xs, 0, x_scales)
+        load_scales(nc.sync, w1s_raw, 0, w1_scales, range(2, 4))
         n3_l = load_list("n3_l", n3)
         two_l = load_list("two_l", two)
         w2w_raw = load_words(nc.sync, "w2w_raw", w2_words, K)
@@ -140,8 +140,9 @@ def tile_picked_tfcdputbmixbond_none_po_kernel(
         w1s = sb("w1s", [P, K], U8)
         deal(nc.vector, w1w[:], w1w_raw[:], LINE // 4)
         xq_scales = pick_scales("xq", offs_l, S)
-        deal(nc.vector, w1s[:], w1s_raw[:], LINE)
         xq_words = pick_words("xq", offs_l, S)
+        deal(nc.vector, w1s[:], w1s_raw[:], LINE, slice(0, 1))
+        deal(nc.vector, w1s[:], w1s_raw[:], LINE, slice(1, PACK))
         for t in range(PACK):
             acc = product(t, w1w, w1s, t, xq_words, xq_scales, [slice(0, S)])
             if t == 0:
@@ -162,9 +163,6 @@ def tile_picked_tfcdputbmixbond_none_po_kernel(
         deal(nc.vector, w2w[:], w2w_raw[:], LINE // 4)
         deal(nc.vector, w2s[:], w2s_raw[:], LINE)
         w3w = sb("w3w", [P, K], I32)
-        w3s = sb("w3s", [P, K], U8)
-        deal(nc.vector, w3w[:], w3w_raw[:], LINE // 4)
-        deal(nc.vector, w3s[:], w3s_raw[:], LINE)
         d = [sb("d%d" % t, [P, S], F32) for t in range(PACK)]
         for t in range(PACK):
             acc = product(PACK + t, w2w, w2s, t, xt_words, xt_scales, [slice(0, S)])
@@ -199,6 +197,9 @@ def tile_picked_tfcdputbmixbond_none_po_kernel(
 
         xc_words_raw, xc_scales_raw = pick("xc", cand_l, C)
         z_rows((0, 1), sb("work_early", [P, 2, 2, S], F32))
+        w3s = sb("w3s", [P, K], U8)
+        deal(nc.vector, w3w[:], w3w_raw[:], LINE // 4)
+        deal(nc.vector, w3s[:], w3s_raw[:], LINE)
         pair_up(slice(0, 2))
         z_rows((2, 3), sb("work_late", [P, 2, 2, S], F32, tag="w2w"))
         pair_up(slice(2, 4))
@@ -223,9 +224,16 @@ def tile_picked_tfcdputbmixbond_none_po_kernel(
 
         halves = [slice(0, S // 2), slice(S // 2, S)]
         z2_grouped = sb("z2_grouped", [P, S, PACK], BF16)
-        for t in range(PACK):
-            for cols in halves if t == PACK - 1 else [slice(0, S)]:
-                nc.vector.tensor_scalar(z2_grouped[:, cols, t], dt_tiles[t][:, cols], gs_t[:, t : t + 1], None, ALU.mult)
+        last = PACK - 1
+        z2_planes = sb("z2_planes", [P, last, S], BF16)
+        for t in range(last):
+            nc.vector.tensor_scalar(z2_planes[:, t, :], dt_tiles[t][:], gs_t[:, t : t + 1], None, ALU.mult)
+        nc.vector.tensor_copy(
+            z2_grouped[:, :, 0:last].rearrange("p (c i) t -> p c t i", i=2),
+            z2_planes[:].rearrange("p t (c i) -> p c t i", i=2),
+        )
+        for cols in halves:
+            nc.vector.tensor_scalar(z2_grouped[:, cols, last], dt_tiles[last][:, cols], gs_t[:, last:PACK], None, ALU.mult)
         z2_words, z2_scales = quantise("z2", z2_grouped, halves)
         b = [sb("b%d" % t, [P, S], F32) for t in range(PACK)]
         for t in range(PACK):

@@ -115,11 +115,10 @@ def tile_picked_tfcdputbmixbond_none_po_kernel(
         w1w_raw = load_words(nc.sync, "w1w_raw", w1_words, K)
         offs_l = load_list("offs_l", offs)
         n1_l = load_list("n1_l", n1)
-        n2_l = load_list("n2_l", n2)
-        load_scales(nc.sync, w1s_raw, 0, w1_scales, range(0, 2))
+        load_scales(nc.sync, w1s_raw, 0, w1_scales)
         xw = load_words(nc.sync, "xw", x_words, T)
         load_scales(nc.sync, xs, 0, x_scales)
-        load_scales(nc.sync, w1s_raw, 0, w1_scales, range(2, 4))
+        n2_l = load_list("n2_l", n2)
         n3_l = load_list("n3_l", n3)
         two_l = load_list("two_l", two)
         w2w_raw = load_words(nc.sync, "w2w_raw", w2_words, K)
@@ -139,10 +138,8 @@ def tile_picked_tfcdputbmixbond_none_po_kernel(
         w1w = sb("w1w", [P, K], I32)
         w1s = sb("w1s", [P, K], U8)
         deal(nc.vector, w1w[:], w1w_raw[:], LINE // 4)
-        xq_scales = pick_scales("xq", offs_l, S)
-        xq_words = pick_words("xq", offs_l, S)
-        deal(nc.vector, w1s[:], w1s_raw[:], LINE, slice(0, 1))
-        deal(nc.vector, w1s[:], w1s_raw[:], LINE, slice(1, PACK))
+        deal(nc.vector, w1s[:], w1s_raw[:], LINE)
+        xq_words, xq_scales = pick("xq", offs_l, S)
         for t in range(PACK):
             acc = product(t, w1w, w1s, t, xq_words, xq_scales, [slice(0, S)])
             if t == 0:
@@ -211,7 +208,10 @@ def tile_picked_tfcdputbmixbond_none_po_kernel(
         a = [sb("a%d" % t, [P, S], F32) for t in range(PACK)]
         for t in range(PACK):
             acc = product(t, w3w, w3s, t, z_words, z_scales, [slice(0, S)])
-            nc.vector.tensor_copy(a[t][:], acc[:])
+            if t < 2:
+                nc.vector.tensor_copy(a[t][:], acc[:])
+            else:
+                nc.scalar.copy(a[t][:], acc[:])
 
         xc_words = sb("xc_words_dealt", [P, C], I32, tag="z_grouped")
         xc_scales = sb("xc_scales_dealt", [P, C], U8, tag="z_planes")
@@ -223,17 +223,10 @@ def tile_picked_tfcdputbmixbond_none_po_kernel(
             fetch(ga[:, t, :], a[t], n6_l)
 
         halves = [slice(0, S // 2), slice(S // 2, S)]
-        z2_grouped = sb("z2_grouped", [P, S, PACK], BF16)
-        last = PACK - 1
-        z2_planes = sb("z2_planes", [P, last, S], BF16)
-        for t in range(last):
-            nc.vector.tensor_scalar(z2_planes[:, t, :], dt_tiles[t][:], gs_t[:, t : t + 1], None, ALU.mult)
-        nc.vector.tensor_copy(
-            z2_grouped[:, :, 0:last].rearrange("p (c i) t -> p c t i", i=2),
-            z2_planes[:].rearrange("p t (c i) -> p c t i", i=2),
-        )
-        for cols in halves:
-            nc.vector.tensor_scalar(z2_grouped[:, cols, last], dt_tiles[last][:, cols], gs_t[:, last:PACK], None, ALU.mult)
+        z2_grouped = sb("z2_grouped", [P, S, PACK], BF16, tag="w3w")
+        for t in range(PACK):
+            for cols in halves if t == PACK - 1 else [slice(0, S)]:
+                nc.vector.tensor_scalar(z2_grouped[:, cols, t], dt_tiles[t][:, cols], gs_t[:, t : t + 1], None, ALU.mult)
         z2_words, z2_scales = quantise("z2", z2_grouped, halves)
         b = [sb("b%d" % t, [P, S], F32) for t in range(PACK)]
         for t in range(PACK):

@@ -205,10 +205,10 @@ def tile_picked_tfcdputbmixbond_none_po_kernel(
             z_grouped[:].rearrange("p (c i) t -> p c t i", i=2), z_planes[:].rearrange("p t (c i) -> p c t i", i=2)
         )
         z_words, z_scales = quantise("z", z_grouped, [slice(0, S)])
-        a = [sb("a%d" % t, [P, S], F32) for t in range(PACK)]
+        a = [sb("a%d" % t, [P, S], F32, tag="rb" if t == PACK - 1 else None) for t in range(PACK)]
         for t in range(PACK):
             acc = product(t, w3w, w3s, t, z_words, z_scales, [slice(0, S)])
-            if t < 2:
+            if t < PACK - 1:
                 nc.vector.tensor_copy(a[t][:], acc[:])
             else:
                 nc.scalar.copy(a[t][:], acc[:])
@@ -218,7 +218,7 @@ def tile_picked_tfcdputbmixbond_none_po_kernel(
         deal(nc.vector, xc_words[:], xc_words_raw[:], LINE // 4)
         deal(nc.vector, xc_scales[:], xc_scales_raw[:], LINE)
 
-        ga = sb("ga", [P, PACK, W], F32)
+        ga = sb("ga", [P, PACK, W], F32, tag="ra")
         for t in range(PACK):
             fetch(ga[:, t, :], a[t], n6_l)
 

from contextlib import ExitStack

import concourse.mybir as mybir

K, T, S, W, C = 512, 2048, 256, 128, 512
FLOPS = 2 * K * 512 * S * 4

F32 = mybir.dt.float32
BF16 = mybir.dt.bfloat16
I32 = mybir.dt.int32
U32 = mybir.dt.uint32
U16 = mybir.dt.uint16
U8 = mybir.dt.uint8
FP8X4 = mybir.dt.float8_e4m3fn_x4
ALU = mybir.AluOpType
COPY = mybir.ActivationFunctionType.Copy

P = 128
PACK = 4
QUADS = 4
LINE = 16


def word_view(dram_words):
    return dram_words[0].rearrange("p n t -> p (n t)").bitcast(I32)


def load_scales(queue, plane, first_row, dram_scales, quads=range(QUADS)):
    for q in quads:
        rows = slice(32 * q + first_row, 32 * q + first_row + 4)
        queue.dma_start(plane[rows, :].bitcast(I32), dram_scales[0, 4 * q : 4 * q + 4, :].bitcast(I32))


def deal(engine, dst, src, run, slots=slice(0, PACK)):
    engine.tensor_copy(
        dst.rearrange("p (t c i) -> p c t i", t=PACK, i=run)[:, :, slots, :],
        src.rearrange("p (c i t) -> p c t i", t=PACK, i=run)[:, :, slots, :],
    )


def tile_picked_tfcdputbmixbond_none_po_kernel(
    tc, x_words, x_scales, w1_words, w1_scales, w2_words, w2_scales, gn, w3_words, w3_scales, gs,
    offs, two, n1, n2, n3, n4, n5, cand, n6, n7, out_0, out_1, out_2,
):
    nc = tc.nc
    with ExitStack() as ctx:
        lists = ctx.enter_context(tc.tile_pool(name="lists", bufs=1))
        keep = ctx.enter_context(tc.tile_pool(name="keep", bufs=1))
        psum = ctx.enter_context(tc.psum_pool(name="psum", bufs=1))

        def sb(name, shape, dtype, tag=None):
            return keep.tile(shape, dtype, name=name, tag=tag or name, align_bytes=64)

        def load_list(name, dram):
            held = lists.tile(list(dram.shape), U16, name=name)
            nc.sync.dma_start(held[:], dram)
            return held

        def load_words(queue, name, dram, width):
            held = sb(name, [P, width], I32)
            queue.dma_start(held[:], word_view(dram))
            return held

        def product(bank, stat_words, stat_scales, t, mov_words, mov_scales, spans):
            acc = psum.tile([P, S], F32, name="acc", tag="bank%d" % bank)
            rows = slice(P * t, P * (t + 1))
            for cols in spans:
                nc.tensor.matmul_mx(
                    acc[:, cols], lhsT=stat_words[:, rows].bitcast(FP8X4), lhsT_scale=stat_scales[:, rows],
                    rhs=mov_words[:, cols].bitcast(FP8X4), rhs_scale=mov_scales[:, cols], start=True, stop=True,
                )
            return acc

        def pick_scales(name, offsets, count):
            scales = sb(name + "_scales", [P, count], U8)
            nc.vector.tensor_copy(scales[:], xs[:].indirect(offsets[:]))
            return scales

        def pick_words(name, offsets, count):
            words = sb(name + "_words", [P, count], I32)
            nc.vector.tensor_copy(words[:].bitcast(U32), xw[:].bitcast(U32).indirect(offsets[:]))
            return words

        def pick(name, offsets, count):
            scales = pick_scales(name, offsets, count)
            return pick_words(name, offsets, count), scales

        def fetch(dst, window, offsets):
            nc.scalar.activation(dst, window[:].indirect(offsets[:]), COPY)

        def put(window, offsets, src):
            nc.scalar.activation(window[:].indirect(offsets[:]), src, COPY)

        def quantise(name, grouped, spans):
            words = sb(name + "_words", [P, S], I32)
            scales = sb(name + "_scales", [P, S], U8)
            for cols in spans:
                nc.vector.quantize_mx(
                    words[:, cols].bitcast(FP8X4), scales[:, cols], grouped[:, cols, :].rearrange("p s t -> p (s t)")
                )
            return words, scales

        xs = sb("xs", [P, T], U8)
        w1s_raw = sb("w1s_raw", [P, K], U8)
        w2s_raw = sb("w2s_raw", [P, K], U8)
        w3s_raw = sb("w3s_raw", [P, K], U8)
        nc.gpsimd.memset(w1s_raw[:].bitcast(I32), 0)
        nc.vector.memset(xs[:].bitcast(I32), 0)
        nc.vector.memset(w2s_raw[:].bitcast(I32), 0)
        nc.vector.memset(w3s_raw[:].bitcast(I32), 0)
        y = [sb("y%d" % t, [P, 2 * S], F32) for t in range(PACK)]
        for t in range(PACK):
            nc.vector.memset(y[t][:, S:], 0.0)

        w1w_raw = load_words(nc.sync, "w1w_raw", w1_words, K)
        offs_l = load_list("offs_l", offs)
        n1_l = load_list("n1_l", n1)
        load_scales(nc.sync, w1s_raw, 0, w1_scales)
        xw = load_words(nc.sync, "xw", x_words, T)
        load_scales(nc.sync, xs, 0, x_scales)
        n2_l = load_list("n2_l", n2)
        n3_l = load_list("n3_l", n3)
        two_l = load_list("two_l", two)
        w2w_raw = load_words(nc.sync, "w2w_raw", w2_words, K)
        load_scales(nc.sync, w2s_raw, 0, w2_scales)
        cand_l = load_list("cand_l", cand)
        gn_t = sb("gn_t", [P, PACK], F32)
        gs_t = sb("gs_t", [P, PACK], F32)
        nc.sync.dma_start(gn_t[:], gn.rearrange("(p t) o -> p (t o)", t=PACK))
        n4_l = load_list("n4_l", n4)
        n5_l = load_list("n5_l", n5)
        w3w_raw = load_words(nc.sync, "w3w_raw", w3_words, K)
        load_scales(nc.sync, w3s_raw, 0, w3_scales)
        nc.sync.dma_start(gs_t[:], gs.rearrange("(p t) o -> p (t o)", t=PACK))
        n6_l = load_list("n6_l", n6)
        n7_l = load_list("n7_l", n7)

        w1w = sb("w1w", [P, K], I32)
        w1s = sb("w1s", [P, K], U8)
        deal(nc.vector, w1w[:], w1w_raw[:], LINE // 4)
        deal(nc.vector, w1s[:], w1s_raw[:], LINE)
        xq_words, xq_scales = pick("xq", offs_l, S)
        for t in range(PACK):
            acc = product(t, w1w, w1s, t, xq_words, xq_scales, [slice(0, S)])
            if t == 0:
                nc.scalar.copy(y[t][:, :S], acc[:])
            else:
                nc.vector.tensor_copy(y[t][:, :S], acc[:])
        g1 = sb("g1", [P, PACK, S], F32)
        g2 = sb("g2", [P, PACK, S], F32)
        g3 = sb("g3", [P, PACK, S], F32)
        for t in range(PACK):
            fetch(g1[:, t, :], y[t], n1_l)
            fetch(g2[:, t, :], y[t], n2_l)
            fetch(g3[:, t, :], y[t], n3_l)

        xt_words, xt_scales = pick("xt", two_l, S)
        w2w = sb("w2w", [P, K], I32)
        w2s = sb("w2s", [P, K], U8)
        deal(nc.vector, w2w[:], w2w_raw[:], LINE // 4)
        deal(nc.vector, w2s[:], w2s_raw[:], LINE)
        w3w = sb("w3w", [P, K], I32)
        d = [sb("d%d" % t, [P, S], F32) for t in range(PACK)]
        for t in range(PACK):
            acc = product(PACK + t, w2w, w2s, t, xt_words, xt_scales, [slice(0, S)])
            nc.vector.tensor_copy(d[t][:], acc[:])
        pa = sb("pa", [P, PACK, W], F32)
        pb = sb("pb", [P, PACK, W], F32)
        ra = sb("ra", [P, PACK, W], F32)
        rb = sb("rb", [P, PACK, W], F32)
        for t in range(PACK):
            fetch(pa[:, t, :], d[t], n4_l)
            fetch(pb[:, t, :], d[t], n5_l)
        dt_tiles = [sb("dt%d" % t, [P, S], F32) for t in range(PACK)]

        def pair_up(pair):
            nc.vector.tensor_tensor(ra[:, pair, :], pa[:, pair, :], pb[:, pair, :], ALU.add)
            nc.vector.tensor_tensor(rb[:, pair, :], pa[:, pair, :], pb[:, pair, :], ALU.mult)
            for t in range(pair.start, pair.stop):
                put(dt_tiles[t], n4_l, ra[:, t, :])
            for t in range(pair.start, pair.stop):
                put(dt_tiles[t], n5_l, rb[:, t, :])

        z_planes = sb("z_planes", [P, PACK, S], BF16)

        def z_rows(planes, work):
            for j, t in enumerate(planes):
                nc.vector.tensor_tensor(work[:, 0, j, :], g2[:, t, :], g3[:, t, :], ALU.max)
                nc.vector.tensor_tensor(work[:, 1, j, :], y[t][:, :S], g1[:, t, :], ALU.max)
            for j, t in enumerate(planes):
                nc.vector.tensor_tensor(work[:, 0, j, :], work[:, 1, j, :], work[:, 0, j, :], ALU.subtract)
            for j, t in enumerate(planes):
                nc.vector.tensor_scalar(z_planes[:, t, :], work[:, 0, j, :], gn_t[:, t : t + 1], None, ALU.mult)

        xc_words_raw, xc_scales_raw = pick("xc", cand_l, C)
        z_rows((0, 1), sb("work_early", [P, 2, 2, S], F32))
        w3s = sb("w3s", [P, K], U8)
        deal(nc.vector, w3w[:], w3w_raw[:], LINE // 4)
        deal(nc.vector, w3s[:], w3s_raw[:], LINE)
        pair_up(slice(0, 2))
        z_rows((2, 3), sb("work_late", [P, 2, 2, S], F32, tag="w2w"))
        pair_up(slice(2, 4))
        z_grouped = sb("z_grouped", [P, S, PACK], BF16)
        nc.vector.tensor_copy(
            z_grouped[:].rearrange("p (c i) t -> p c t i", i=2), z_planes[:].rearrange("p t (c i) -> p c t i", i=2)
        )
        z_words, z_scales = quantise("z", z_grouped, [slice(0, S)])
        a = [sb("a%d" % t, [P, S], F32, tag="rb" if t == PACK - 1 else None) for t in range(PACK)]
        for t in range(PACK):
            acc = product(t, w3w, w3s, t, z_words, z_scales, [slice(0, S)])
            if t < PACK - 1:
                nc.vector.tensor_copy(a[t][:], acc[:])
            else:
                nc.scalar.copy(a[t][:], acc[:])

        xc_words = sb("xc_words_dealt", [P, C], I32, tag="z_grouped")
        xc_scales = sb("xc_scales_dealt", [P, C], U8, tag="z_planes")
        deal(nc.vector, xc_words[:], xc_words_raw[:], LINE // 4)
        deal(nc.vector, xc_scales[:], xc_scales_raw[:], LINE)

        ga = sb("ga", [P, PACK, W], F32, tag="ra")
        for t in range(PACK):
            fetch(ga[:, t, :], a[t], n6_l)

        halves = [slice(0, S // 2), slice(S // 2, S)]
        z2_grouped = sb("z2_grouped", [P, S, PACK], BF16, tag="w3w")
        for t in range(PACK):
            for cols in halves if t == PACK - 1 else [slice(0, S)]:
                nc.vector.tensor_scalar(z2_grouped[:, cols, t], dt_tiles[t][:, cols], gs_t[:, t : t + 1], None, ALU.mult)
        z2_words, z2_scales = quantise("z2", z2_grouped, halves)
        b = [sb("b%d" % t, [P, S], F32) for t in range(PACK)]
        for t in range(PACK):
            acc = product(PACK + t, xc_words, xc_scales, t, z2_words, z2_scales, halves)
            if t == 0:
                nc.scalar.activation(b[t][:], acc[:], COPY, scale=0.0625)
            else:
                nc.vector.tensor_scalar(b[t][:], acc[:], 0.0625, None, ALU.mult)

        gb = sb("gb", [P, PACK, W], F32)
        ra2 = sb("ra2", [P, PACK, W], F32)
        out_grouped = sb("out_grouped", [P, S, PACK], BF16)
        out_rows = out_0.rearrange("(p t) s -> p t s", t=PACK)
        for t in range(PACK):
            fetch(gb[:, t, :], b[t], n7_l)
            nc.vector.scalar_tensor_tensor(ra2[:, t, :], ga[:, t, :], -0.5, gb[:, t, :], ALU.mult, ALU.add)
            put(a[t], n6_l, ra2[:, t, :])
        for t in range(PACK):
            nc.sync.dma_start(out_rows[:, t, :], a[t][:])
            for cols in halves if t == PACK - 1 else [slice(0, S)]:
                nc.vector.tensor_copy(out_grouped[:, cols, t], a[t][:, cols])
        out_words, out_scales = quantise("out", out_grouped, halves)
        nc.sync.dma_start(word_view(out_1), out_words[:])
        for q in range(QUADS):
            queue = nc.scalar if q % 2 == 0 else nc.sync
            queue.dma_start(out_2[0, 4 * q : 4 * q + 4, :].bitcast(I32), out_scales[32 * q : 32 * q + 4, :].bitcast(I32))
